import numpy as np, ml_dtypes
CORES = [24,26,29,31,48,50,53,55]
N = 8
def setup_inputs(rng):
    dy = rng.standard_normal((N, 128, N * 128), dtype=np.float32).astype(ml_dtypes.bfloat16)
    dyt = np.concatenate([dy[:, :, 128 * j:128 * j + 128].transpose(0, 2, 1) for j in range(N)], axis=2)
    return {"x": rng.standard_normal((N, 128, 128), dtype=np.float32).astype(ml_dtypes.bfloat16), "wt": rng.standard_normal((N, 128, 128), dtype=np.float32).astype(ml_dtypes.bfloat16), "dy": dy, "dyt": dyt}
def setup_inputs_big(rng):
    d = setup_inputs(rng)
    for k in ("x", "wt", "dy", "dyt"): d[k] = (d[k].astype(np.float32) * 1024.0).astype(d[k].dtype)
    return d
def setup_inputs_small(rng):
    d = setup_inputs(rng)
    for k in ("x", "wt", "dy", "dyt"): d[k] = (d[k].astype(np.float32) * (1 / 1024.0)).astype(d[k].dtype)
    return d
def setup_inputs_apart(rng):
    d = setup_inputs(rng)
    f = (10.0 ** rng.permutation(np.linspace(-1.5, 1.5, N))).astype(np.float32).reshape(N, 1, 1)
    for k in ("x", "wt", "dy", "dyt"): d[k] = (d[k].astype(np.float32) * f).astype(d[k].dtype)
    return d
def reference(x, wt, dy, dyt):
    X, WT, DY, DYT = x.astype(np.float64), wt.astype(np.float64), dy.astype(np.float64), dyt.astype(np.float64)
    dx = np.zeros((N, 128, 128)); dw = np.zeros((N, 128, 128))
    for r in range(N):
        for j in range(N):
            dx[r] += WT[j].T @ DY[j][:, 128 * r:128 * r + 128]
            dw[r] += X[j].T @ DYT[r][:, 128 * j:128 * j + 128]
    return {"dx": dx.astype(ml_dtypes.bfloat16), "dw": dw.astype(ml_dtypes.bfloat16)}

@@ -1,0 +1,227 @@
+from concourse.bass import DstId, RemoteDMATransfer
+from concourse.mybir import AluOpType
+
+B = 128
+
+SCRATCH = {
+    "xs": ("sbuf", [128, 8 * B], "bfloat16"),
+    "wts": ("sbuf", [128, B], "bfloat16"),
+    "dys": ("sbuf", [128, 8 * B], "bfloat16"),
+    "dyts": ("sbuf", [128, 8 * B], "bfloat16"),
+    "ps": ("sbuf", [128, 8 * B], "bfloat16"),
+    "gl": ("sbuf", [128, 6 * B], "bfloat16"),
+    "pl": ("sbuf", [128, 3 * B], "bfloat16"),
+    "sl": ("sbuf", [128, B], "bfloat16"),
+    "t0": ("sbuf", [128, B], "float32"),
+    "t1": ("sbuf", [128, B], "float32"),
+    "t2": ("sbuf", [128, B], "float32"),
+    "dxs": ("sbuf", [128, B], "bfloat16"),
+    "dws": ("sbuf", [128, B], "bfloat16"),
+    "pfa": ("psum", [128, 512], "float32"),
+    "pfb": ("psum", [128, 512], "float32"),
+    "pn": ("psum", [128, 512], "float32"),
+    "pw": ("psum", [128, 512], "float32"),
+}
+SEMAPHORES = (["xl", "wl", "dya", "dyb", "dyn", "dtn", "dtf", "mfa", "mfb", "mn", "mw", "cfa", "cfb", "cn", "cw", "cx",
+               "v0", "v1", "v2", "xp", "ga", "pa", "sa", "stx", "stw", "sent"] + ["xa%d" % s for s in range(8)])
+
+
+def _bits(m):
+    return [1 << i for i in range(m.bit_length()) if (m >> i) & 1]
+
+
+def _join(bs):
+    r = 0
+    for b in bs:
+        r |= b
+    return r
+
+
+def _layout(T, topo):
+    cores = list(T.cores)
+    chips = sorted(set(topo.chip(c) for c in cores))
+    mem = dict((ch, [c for c in cores if topo.chip(c) == ch]) for ch in chips)
+    far = {chips[0]: chips[1], chips[1]: chips[0]}
+    gate, inner, slot = {}, {}, {}
+    dies = sorted(set(topo.die(c) for c in cores))
+    for i, ch in enumerate(chips):
+        for c in mem[ch]:
+            ok = all(topo.may_write(c, f) for f in mem[far[ch]])
+            (gate if ok else inner)[(ch, topo.die(c))] = c
+        for k, c in enumerate([inner[(ch, d)] for d in dies] + [gate[(ch, d)] for d in dies]):
+            slot[c] = 4 * i + k
+    return dict(mem=mem, far=far, gate=gate, inner=inner, slot=slot, dies=dies)
+
+
+def _groups(c, L, topo):
+    d = topo.die(c)
+    od = [x for x in L["dies"] if x != d][0]
+    return (od, d) if L["gate"][(topo.chip(c), d)] == c else (d, od)
+
+
+def _calls(c, L, topo):
+    mem, gate, inner, slot = L["mem"], L["gate"], L["inner"], L["slot"]
+    ch, d = topo.chip(c), topo.die(c)
+    fch = L["far"][ch]
+    od = [x for x in L["dies"] if x != d][0]
+    mates = [m for m in mem[ch] if m != c]
+    on = _bits(topo.mask(c, mates[0]))
+
+    def idx(dst, src):
+        return [m for m in mem[topo.chip(dst)] if m != dst].index(src)
+
+    def xt(s, n=1):
+        return ("xs", B * s, B * (s + n))
+
+    def bcast(s, n, dsts, eng, sem):
+        return ([xt(s, n)], [(m,) + xt(s, n) for m in dsts], _join(eng), sem, 0)
+
+    def to_gate(k, gt, eng):
+        return ([("ps", 2 * B * k, 2 * B * (k + 1))], [(gt, "gl", 2 * B * idx(gt, c), 2 * B * (idx(gt, c) + 1))],
+                _join(eng), "ga", 0)
+
+    def near(eng):
+        h = len(eng) // 2
+        parts = [eng[:h], eng[h:h + h // 2], eng[h + h // 2:]]
+        return [([("ps", B * (4 + mem[ch].index(m)), B * (5 + mem[ch].index(m)))],
+                 [(m, "pl", B * idx(m, c), B * (idx(m, c) + 1))], _join(p), "pa", 0) for m, p in zip(mates, parts)]
+
+    me = "xa%d" % slot[c]
+    if gate[(ch, d)] == c:
+        out = _bits(topo.mask(c, mem[fch][0]))
+        loc = [b for b in on if b not in out]
+        fg = [r for r in mem[fch] if topo.die(r) == d]
+        pair = [slot[inner[(ch, x)]] for x in L["dies"]]
+        h = len(out) // 2
+        folds = [([("gl", B * (2 * k + p), B * (2 * k + p + 1)) for k in range(3)] + [("ps", B * (2 + p), B * (3 + p))],
+                  [(r, "sl", 0, B)], _join(e), "sa", 1) for p, (r, e) in enumerate(zip(fg, (out[:h], out[h:])))]
+        return [
+            ([("xl", 16)], [bcast(slot[c], 1, [inner[(fch, d)]], out, me), bcast(slot[c], 1, mates, loc, me)]),
+            ([("cfa", 1)], [to_gate(0, gate[(ch, od)], loc)]),
+            ([("xa%d" % s, None) for s in pair], [bcast(min(pair), 2, fg, out, "xp")]),
+            ([("cn", 1)], near(loc)),
+            ([("ga", None), ("cfb", 1)], folds),
+        ]
+    h = len(on) // 2
+    fs = slot[gate[(fch, d)]]
+    return [
+        ([("xl", 16)], [bcast(slot[c], 1, mates, on, me)]),
+        ([("cfa", 1), ("cfb", 1)], [to_gate(0, gate[(ch, d)], on[:h]), to_gate(1, gate[(ch, od)], on[h:])]),
+        ([("cn", 1)], near(on)),
+        ([("xa%d" % fs, None)], [bcast(fs, 1, mates, on, "xa%d" % fs)]),
+    ]
+
+
+def rank_program(g, core, T, topo):
+    rank = T.rank_of(core)
+    if rank is None:
+        return
+    L = _layout(T, topo)
+    mem, gate, inner, slot = L["mem"], L["gate"], L["inner"], L["slot"]
+    ch, d = topo.chip(core), topo.die(core)
+    fch = L["far"][ch]
+    S = T.sem
+    te, ve, sy, sc = g.tensor, g.vector, g.sync, g.scalar
+
+    arr, sent = {}, 0
+    for c in T.cores:
+        for _, trs in _calls(c, L, topo):
+            for _, dsts, mask, sem, _ in trs:
+                n = len(_bits(mask))
+                if c == core:
+                    sent += n
+                for dst in dsts:
+                    arr[(dst[0], sem)] = arr.get((dst[0], sem), 0) + n
+
+    def cols(ranks):
+        lo = min(ranks)
+        assert sorted(ranks) == list(range(lo, lo + len(ranks)))
+        return slice(B * lo, B * (lo + len(ranks)))
+
+    da, db = _groups(core, L, topo)
+    ca = cols([T.rank_of(r) for r in mem[fch] if topo.die(r) == da])
+    cb = cols([T.rank_of(r) for r in mem[fch] if topo.die(r) == db])
+    cnear = cols([T.rank_of(r) for r in mem[ch]])
+    cfar = cols([T.rank_of(r) for r in mem[fch]])
+
+    def xs(c):
+        return T.xs[:, B * slot[c]:B * (slot[c] + 1)]
+
+    def dyt(c):
+        return T.dyts[:, B * T.rank_of(c):B * (T.rank_of(c) + 1)]
+
+    sy.dma_start(xs(core), T.x[:]).then_inc(S.xl, 16)
+    sc.dma_start(T.wts[:], T.wt[:]).then_inc(S.wl, 16)
+    sy.dma_start(T.dys[:, ca], T.dy[:, ca]).then_inc(S.dya, 16)
+    sc.dma_start(T.dys[:, cb], T.dy[:, cb]).then_inc(S.dyb, 16)
+    sy.dma_start(T.dys[:, cnear], T.dy[:, cnear]).then_inc(S.dyn, 16)
+    sc.dma_start(T.dyts[:, cnear], T.dyt[:, cnear]).then_inc(S.dtn, 16)
+    sy.dma_start(T.dyts[:, cfar], T.dyt[:, cfar]).then_inc(S.dtf, 16)
+
+    te.wait_ge(S.wl, 16)
+    te.wait_ge(S.dya, 16)
+    te.matmul(T.pfa[:, 0:2 * B], T.wts[:], T.dys[:, ca], True, True).then_inc(S.mfa, 1)
+    te.wait_ge(S.dyb, 16)
+    te.matmul(T.pfb[:, 0:2 * B], T.wts[:], T.dys[:, cb], True, True).then_inc(S.mfb, 1)
+    te.wait_ge(S.dyn, 16)
+    te.matmul(T.pn[:, 0:4 * B], T.wts[:], T.dys[:, cnear], True, True).then_inc(S.mn, 1)
+    te.wait_ge(S.xl, 16)
+    te.wait_ge(S.dtn, 16)
+    te.matmul(T.pw[:, 0:B], xs(core), dyt(core), True, False)
+    for m in mem[ch]:
+        if m != core:
+            te.wait_ge(S["xa%d" % slot[m]], arr[(core, "xa%d" % slot[m])])
+            te.matmul(T.pw[:, 0:B], xs(m), dyt(m), False, False)
+    te.wait_ge(S.dtf, 16)
+    fgates = [gate[(fch, x)] for x in L["dies"]]
+    direct = [f for f in fgates if inner[(ch, topo.die(f))] == core]
+    passed = [f for f in fgates if f not in direct]
+    for f in direct:
+        te.wait_ge(S["xa%d" % slot[f]], arr[(core, "xa%d" % slot[f])])
+        te.matmul(T.pw[:, 0:B], xs(f), dyt(f), False, False)
+    te.wait_ge(S.xp, arr[(core, "xp")])
+    for x in L["dies"]:
+        te.matmul(T.pw[:, 0:B], xs(inner[(fch, x)]), dyt(inner[(fch, x)]), False, False)
+    for k, f in enumerate(passed):
+        te.wait_ge(S["xa%d" % slot[f]], arr[(core, "xa%d" % slot[f])])
+        mm = te.matmul(T.pw[:, 0:B], xs(f), dyt(f), False, k == len(passed) - 1)
+    mm.then_inc(S.mw, 1)
+
+    ve.wait_ge(S.mfa, 1)
+    ve.tensor_copy(T.ps[:, 0:2 * B], T.pfa[:, 0:2 * B]).then_inc(S.cfa, 1)
+    ve.wait_ge(S.mfb, 1)
+    ve.tensor_copy(T.ps[:, 2 * B:4 * B], T.pfb[:, 0:2 * B]).then_inc(S.cfb, 1)
+    ve.wait_ge(S.mn, 1)
+    ve.tensor_copy(T.ps[:, 4 * B:8 * B], T.pn[:, 0:4 * B]).then_inc(S.cn, 1)
+    own = mem[ch].index(core)
+    ve.wait_ge(S.pa, arr[(core, "pa")])
+    ve.tensor_tensor(T.t0[:], T.pn[:, B * own:B * (own + 1)], T.pl[:, 0:B], AluOpType.add).then_inc(S.v0, 1)
+    ve.tensor_tensor(T.t1[:], T.pl[:, B:2 * B], T.pl[:, 2 * B:3 * B], AluOpType.add).then_inc(S.v1, 1)
+    ve.wait_ge(S.v0, 1)
+    ve.wait_ge(S.v1, 1)
+    ve.tensor_tensor(T.t2[:], T.t0[:], T.t1[:], AluOpType.add).then_inc(S.v2, 1)
+    ve.wait_ge(S.mw, 1)
+    ve.tensor_copy(T.dws[:], T.pw[:, 0:B]).then_inc(S.cw, 1)
+    ve.wait_ge(S.v2, 1)
+    ve.wait_ge(S.sa, arr[(core, "sa")])
+    ve.tensor_tensor(T.dxs[:], T.t2[:], T.sl[:], AluOpType.add).then_inc(S.cx, 1)
+
+    sc.wait_ge(S.cw, 1)
+    sc.dma_start(T.dw[:], T.dws[:]).then_inc(S.stw, 16)
+    sc.wait_ge(S.stw, 16)
+    sy.wait_ge(S.cx, 1)
+    sy.dma_start(T.dx[:], T.dxs[:]).then_inc(S.stx, 16)
+    sy.wait_ge(S.stx, 16)
+
+    def ap(spec):
+        return T[spec[0]][:, spec[1]:spec[2]]
+
+    for waits, trs in _calls(core, L, topo):
+        for sem, val in waits:
+            g.wait_ge(S[sem], arr[(core, sem)] if val is None else val)
+        g.remote_dma_fused(
+            [RemoteDMATransfer(dst_ids=[DstId(rid=topo.addr(t[0])[0], pnc=topo.addr(t[0])[1]) for t in dsts],
+                               dma_engine_mask=mask, remote_sem=S[sem], srcs=[ap(s) for s in srcs],
+                               dsts=[ap(t[1:]) for t in dsts], alu_op=alu)
+             for srcs, dsts, mask, sem, alu in trs], local_sem=S.sent)
+    g.wait_ge(S.sent, sent)

@@ -1,5 +1,5 @@
 from concourse.bass import DstId, RemoteDMATransfer
-from concourse.mybir import AluOpType
+from concourse.mybir import AluOpType, ActivationFunctionType
 
 B = 128
 
@@ -14,16 +14,17 @@ SCRATCH = {
     "sl": ("sbuf", [128, B], "bfloat16"),
     "t0": ("sbuf", [128, B], "float32"),
     "t1": ("sbuf", [128, B], "float32"),
-    "t2": ("sbuf", [128, B], "float32"),
     "dxs": ("sbuf", [128, B], "bfloat16"),
     "dws": ("sbuf", [128, B], "bfloat16"),
-    "pfa": ("psum", [128, 512], "float32"),
-    "pfb": ("psum", [128, 512], "float32"),
+    "pf0": ("psum", [128, 512], "float32"),
+    "pf1": ("psum", [128, 512], "float32"),
     "pn": ("psum", [128, 512], "float32"),
+    "pt": ("psum", [128, 512], "float32"),
     "pw": ("psum", [128, 512], "float32"),
 }
-SEMAPHORES = (["xl", "wl", "dya", "dyb", "dyn", "dtn", "dtf", "mfa", "mfb", "mn", "mw", "cfa", "cfb", "cn", "cw", "cx",
-               "v0", "v1", "v2", "xp", "ga", "pa", "sa", "stx", "stw", "sent"] + ["xa%d" % s for s in range(8)])
+SEMAPHORES = (["xl", "wl", "dy0", "dy1", "dyn", "dtn", "dtf", "mf0", "mf1", "mn", "mw", "cf0", "cf1", "cn", "cw", "cx",
+               "v0", "v1", "v2", "ga", "pa", "sa", "stx", "stw", "sent"]
+              + ["xa%d" % s for s in range(8)] + ["xb%d" % s for s in range(8)])
 
 
 def _bits(m):
@@ -48,37 +49,36 @@ def _layout(T, topo):
         for c in mem[ch]:
             ok = all(topo.may_write(c, f) for f in mem[far[ch]])
             (gate if ok else inner)[(ch, topo.die(c))] = c
-        for k, c in enumerate([inner[(ch, d)] for d in dies] + [gate[(ch, d)] for d in dies]):
-            slot[c] = 4 * i + k
+        for k, x in enumerate(dies):
+            slot[inner[(ch, x)]] = 4 * i + 2 * k
+            slot[gate[(ch, x)]] = 4 * i + 2 * k + 1
     return dict(mem=mem, far=far, gate=gate, inner=inner, slot=slot, dies=dies)
 
 
-def _groups(c, L, topo):
-    d = topo.die(c)
-    od = [x for x in L["dies"] if x != d][0]
-    return (od, d) if L["gate"][(topo.chip(c), d)] == c else (d, od)
-
-
 def _calls(c, L, topo):
-    mem, gate, inner, slot = L["mem"], L["gate"], L["inner"], L["slot"]
+    mem, gate, inner, slot, dies = L["mem"], L["gate"], L["inner"], L["slot"], L["dies"]
     ch, d = topo.chip(c), topo.die(c)
     fch = L["far"][ch]
-    od = [x for x in L["dies"] if x != d][0]
+    od = [x for x in dies if x != d][0]
+    kd, ko = dies.index(d), dies.index(od)
     mates = [m for m in mem[ch] if m != c]
+    I, G = inner[(ch, d)], gate[(ch, d)]
+    FI, FG = inner[(fch, d)], gate[(fch, d)]
     on = _bits(topo.mask(c, mates[0]))
 
     def idx(dst, src):
         return [m for m in mem[topo.chip(dst)] if m != dst].index(src)
 
-    def xt(s, n=1):
+    def xt(s, n):
         return ("xs", B * s, B * (s + n))
 
-    def bcast(s, n, dsts, eng, sem):
-        return ([xt(s, n)], [(m,) + xt(s, n) for m in dsts], _join(eng), sem, 0)
+    def cp(s, n, dsts, eng):
+        return ([xt(s, n)], [(m,) + xt(s, n) for m in dsts], _join(eng), ("xa%d" if n == 1 else "xb%d") % s, 0)
 
-    def to_gate(k, gt, eng):
-        return ([("ps", 2 * B * k, 2 * B * (k + 1))], [(gt, "gl", 2 * B * idx(gt, c), 2 * B * (idx(gt, c) + 1))],
-                _join(eng), "ga", 0)
+    def grp(k, eng):
+        gt = gate[(ch, dies[k])]
+        j = idx(gt, c)
+        return ([("ps", 2 * B * k, 2 * B * (k + 1))], [(gt, "gl", 2 * B * j, 2 * B * (j + 1))], _join(eng), "ga", 0)
 
     def near(eng):
         h = len(eng) // 2
@@ -86,29 +86,28 @@ def _calls(c, L, topo):
         return [([("ps", B * (4 + mem[ch].index(m)), B * (5 + mem[ch].index(m)))],
                  [(m, "pl", B * idx(m, c), B * (idx(m, c) + 1))], _join(p), "pa", 0) for m, p in zip(mates, parts)]
 
-    me = "xa%d" % slot[c]
-    if gate[(ch, d)] == c:
-        out = _bits(topo.mask(c, mem[fch][0]))
+    if G == c:
+        out = _bits(topo.mask(c, FI))
         loc = [b for b in on if b not in out]
-        fg = [r for r in mem[fch] if topo.die(r) == d]
-        pair = [slot[inner[(ch, x)]] for x in L["dies"]]
         h = len(out) // 2
-        folds = [([("gl", B * (2 * k + p), B * (2 * k + p + 1)) for k in range(3)] + [("ps", B * (2 + p), B * (3 + p))],
+        fg = [r for r in mem[fch] if topo.die(r) == d]
+        folds = [([("gl", B * (2 * j + p), B * (2 * j + p + 1)) for j in range(3)]
+                  + [("ps", B * (2 * kd + p), B * (2 * kd + p + 1))],
                   [(r, "sl", 0, B)], _join(e), "sa", 1) for p, (r, e) in enumerate(zip(fg, (out[:h], out[h:])))]
         return [
-            ([("xl", 16)], [bcast(slot[c], 1, [inner[(fch, d)]], out, me), bcast(slot[c], 1, mates, loc, me)]),
-            ([("cfa", 1)], [to_gate(0, gate[(ch, od)], loc)]),
-            ([("xa%d" % s, None) for s in pair], [bcast(min(pair), 2, fg, out, "xp")]),
+            ([("xl", 16)], [cp(slot[c], 1, [FI], out), cp(slot[c], 1, [I], loc)]),
+            ([("cf%d" % ko, 1)], [grp(ko, loc)]),
+            ([("xa%d" % slot[I], None)], [cp(slot[I], 1, [FI], out)]),
             ([("cn", 1)], near(loc)),
-            ([("ga", None), ("cfb", 1)], folds),
+            ([("ga", None), ("cf%d" % kd, 1)], folds),
         ]
-    h = len(on) // 2
-    fs = slot[gate[(fch, d)]]
+    ea, eb = on[0::2], on[1::2]
     return [
-        ([("xl", 16)], [bcast(slot[c], 1, mates, on, me)]),
-        ([("cfa", 1), ("cfb", 1)], [to_gate(0, gate[(ch, d)], on[:h]), to_gate(1, gate[(ch, od)], on[h:])]),
+        ([("xl", 16)], [cp(slot[c], 1, [G], eb)]),
+        ([("cf%d" % ko, 1), ("cf%d" % kd, 1)], [grp(ko, ea), grp(kd, eb)]),
+        ([("xa%d" % slot[G], None)], [cp(slot[c], 2, [m for m in mates if topo.die(m) == od], on)]),
         ([("cn", 1)], near(on)),
-        ([("xa%d" % fs, None)], [bcast(fs, 1, mates, on, "xa%d" % fs)]),
+        ([("xa%d" % slot[FG], None), ("xa%d" % slot[FI], None)], [cp(slot[FI], 2, mates, on)]),
     ]
 
 
@@ -117,9 +116,12 @@ def rank_program(g, core, T, topo):
     if rank is None:
         return
     L = _layout(T, topo)
-    mem, gate, inner, slot = L["mem"], L["gate"], L["inner"], L["slot"]
+    mem, gate, inner, slot, dies = L["mem"], L["gate"], L["inner"], L["slot"], L["dies"]
     ch, d = topo.chip(core), topo.die(core)
     fch = L["far"][ch]
+    od = [x for x in dies if x != d][0]
+    kd, ko = dies.index(d), dies.index(od)
+    is_gate = gate[(ch, d)] == core
     S = T.sem
     te, ve, sy, sc = g.tensor, g.vector, g.sync, g.scalar
 
@@ -133,64 +135,63 @@ def rank_program(g, core, T, topo):
                 for dst in dsts:
                     arr[(dst[0], sem)] = arr.get((dst[0], sem), 0) + n
 
-    def cols(ranks):
+    def cols(cs):
+        ranks = [T.rank_of(c) for c in cs]
         lo = min(ranks)
-        assert sorted(ranks) == list(range(lo, lo + len(ranks)))
+        assert ranks == list(range(lo, lo + len(ranks)))
         return slice(B * lo, B * (lo + len(ranks)))
 
-    da, db = _groups(core, L, topo)
-    ca = cols([T.rank_of(r) for r in mem[fch] if topo.die(r) == da])
-    cb = cols([T.rank_of(r) for r in mem[fch] if topo.die(r) == db])
-    cnear = cols([T.rank_of(r) for r in mem[ch]])
-    cfar = cols([T.rank_of(r) for r in mem[fch]])
+    cnear, cfar = cols(mem[ch]), cols(mem[fch])
+    cf = [cols([r for r in mem[fch] if topo.die(r) == x]) for x in dies]
+    by_slot = dict((s, c) for c, s in slot.items())
 
-    def xs(c):
-        return T.xs[:, B * slot[c]:B * (slot[c] + 1)]
+    def xs(s):
+        return T.xs[:, B * s:B * (s + 1)]
 
-    def dyt(c):
-        return T.dyts[:, B * T.rank_of(c):B * (T.rank_of(c) + 1)]
+    def dyt(s):
+        r = T.rank_of(by_slot[s])
+        return T.dyts[:, B * r:B * (r + 1)]
 
-    sy.dma_start(xs(core), T.x[:]).then_inc(S.xl, 16)
+    sy.dma_start(xs(slot[core]), T.x[:]).then_inc(S.xl, 16)
     sc.dma_start(T.wts[:], T.wt[:]).then_inc(S.wl, 16)
-    sy.dma_start(T.dys[:, ca], T.dy[:, ca]).then_inc(S.dya, 16)
-    sc.dma_start(T.dys[:, cb], T.dy[:, cb]).then_inc(S.dyb, 16)
+    sy.dma_start(T.dys[:, cf[ko]], T.dy[:, cf[ko]]).then_inc(S["dy%d" % ko], 16)
+    sc.dma_start(T.dys[:, cf[kd]], T.dy[:, cf[kd]]).then_inc(S["dy%d" % kd], 16)
     sy.dma_start(T.dys[:, cnear], T.dy[:, cnear]).then_inc(S.dyn, 16)
     sc.dma_start(T.dyts[:, cnear], T.dyt[:, cnear]).then_inc(S.dtn, 16)
     sy.dma_start(T.dyts[:, cfar], T.dyt[:, cfar]).then_inc(S.dtf, 16)
 
     te.wait_ge(S.wl, 16)
-    te.wait_ge(S.dya, 16)
-    te.matmul(T.pfa[:, 0:2 * B], T.wts[:], T.dys[:, ca], True, True).then_inc(S.mfa, 1)
-    te.wait_ge(S.dyb, 16)
-    te.matmul(T.pfb[:, 0:2 * B], T.wts[:], T.dys[:, cb], True, True).then_inc(S.mfb, 1)
+    for k in (ko, kd):
+        te.wait_ge(S["dy%d" % k], 16)
+        te.matmul(T["pf%d" % k][:, 0:2 * B], T.wts[:], T.dys[:, cf[k]], True, True).then_inc(S["mf%d" % k], 1)
     te.wait_ge(S.dyn, 16)
     te.matmul(T.pn[:, 0:4 * B], T.wts[:], T.dys[:, cnear], True, True).then_inc(S.mn, 1)
+
+    sI, sG = slot[inner[(ch, d)]], slot[gate[(ch, d)]]
+    sO = slot[inner[(ch, od)]]
+    fD, fO = slot[inner[(fch, d)]], slot[inner[(fch, od)]]
+    if is_gate:
+        due = [("xa%d" % sI, [sI]), ("xb%d" % sO, [sO, sO + 1]), ("xb%d" % fD, [fD, fD + 1]),
+               ("xb%d" % fO, [fO, fO + 1])]
+    else:
+        due = [("xa%d" % sG, [sG]), ("xb%d" % sO, [sO, sO + 1]), ("xa%d" % (fD + 1), [fD + 1]), ("xa%d" % fD, [fD]),
+               ("xb%d" % fO, [fO, fO + 1])]
     te.wait_ge(S.xl, 16)
     te.wait_ge(S.dtn, 16)
-    te.matmul(T.pw[:, 0:B], xs(core), dyt(core), True, False)
-    for m in mem[ch]:
-        if m != core:
-            te.wait_ge(S["xa%d" % slot[m]], arr[(core, "xa%d" % slot[m])])
-            te.matmul(T.pw[:, 0:B], xs(m), dyt(m), False, False)
-    te.wait_ge(S.dtf, 16)
-    fgates = [gate[(fch, x)] for x in L["dies"]]
-    direct = [f for f in fgates if inner[(ch, topo.die(f))] == core]
-    passed = [f for f in fgates if f not in direct]
-    for f in direct:
-        te.wait_ge(S["xa%d" % slot[f]], arr[(core, "xa%d" % slot[f])])
-        te.matmul(T.pw[:, 0:B], xs(f), dyt(f), False, False)
-    te.wait_ge(S.xp, arr[(core, "xp")])
-    for x in L["dies"]:
-        te.matmul(T.pw[:, 0:B], xs(inner[(fch, x)]), dyt(inner[(fch, x)]), False, False)
-    for k, f in enumerate(passed):
-        te.wait_ge(S["xa%d" % slot[f]], arr[(core, "xa%d" % slot[f])])
-        mm = te.matmul(T.pw[:, 0:B], xs(f), dyt(f), False, k == len(passed) - 1)
+    te.matmul(T.pw[:, 0:B], xs(slot[core]), dyt(slot[core]), True, False)
+    far_seen = False
+    for n, (sem, ss) in enumerate(due):
+        if not far_seen and topo.chip(by_slot[ss[0]]) != ch:
+            te.wait_ge(S.dtf, 16)
+            far_seen = True
+        te.wait_ge(S[sem], arr[(core, sem)])
+        for s in ss:
+            mm = te.matmul(T.pw[:, 0:B], xs(s), dyt(s), False, n == len(due) - 1 and s == ss[-1])
     mm.then_inc(S.mw, 1)
 
-    ve.wait_ge(S.mfa, 1)
-    ve.tensor_copy(T.ps[:, 0:2 * B], T.pfa[:, 0:2 * B]).then_inc(S.cfa, 1)
-    ve.wait_ge(S.mfb, 1)
-    ve.tensor_copy(T.ps[:, 2 * B:4 * B], T.pfb[:, 0:2 * B]).then_inc(S.cfb, 1)
+    for k in (ko, kd):
+        ve.wait_ge(S["mf%d" % k], 1)
+        ve.tensor_copy(T.ps[:, 2 * B * k:2 * B * (k + 1)], T["pf%d" % k][:, 0:2 * B]).then_inc(S["cf%d" % k], 1)
     ve.wait_ge(S.mn, 1)
     ve.tensor_copy(T.ps[:, 4 * B:8 * B], T.pn[:, 0:4 * B]).then_inc(S.cn, 1)
     own = mem[ch].index(core)
@@ -199,13 +200,13 @@ def rank_program(g, core, T, topo):
     ve.tensor_tensor(T.t1[:], T.pl[:, B:2 * B], T.pl[:, 2 * B:3 * B], AluOpType.add).then_inc(S.v1, 1)
     ve.wait_ge(S.v0, 1)
     ve.wait_ge(S.v1, 1)
-    ve.tensor_tensor(T.t2[:], T.t0[:], T.t1[:], AluOpType.add).then_inc(S.v2, 1)
-    ve.wait_ge(S.mw, 1)
-    ve.tensor_copy(T.dws[:], T.pw[:, 0:B]).then_inc(S.cw, 1)
+    ve.tensor_tensor(T.pt[:, 0:B], T.t0[:], T.t1[:], AluOpType.add).then_inc(S.v2, 1)
     ve.wait_ge(S.v2, 1)
     ve.wait_ge(S.sa, arr[(core, "sa")])
-    ve.tensor_tensor(T.dxs[:], T.t2[:], T.sl[:], AluOpType.add).then_inc(S.cx, 1)
+    ve.tensor_tensor(T.dxs[:], T.pt[:, 0:B], T.sl[:], AluOpType.add).then_inc(S.cx, 1)
 
+    sc.wait_ge(S.mw, 1)
+    sc.activation(T.dws[:], T.pw[:, 0:B], ActivationFunctionType.Copy).then_inc(S.cw, 1)
     sc.wait_ge(S.cw, 1)
     sc.dma_start(T.dw[:], T.dws[:]).then_inc(S.stw, 16)
     sc.wait_ge(S.stw, 16)

from concourse.bass import DstId, RemoteDMATransfer
from concourse.mybir import AluOpType, ActivationFunctionType

B = 128

SCRATCH = {
    "xs": ("sbuf", [128, 8 * B], "bfloat16"),
    "wts": ("sbuf", [128, B], "bfloat16"),
    "dys": ("sbuf", [128, 8 * B], "bfloat16"),
    "dyts": ("sbuf", [128, 8 * B], "bfloat16"),
    "ps": ("sbuf", [128, 8 * B], "bfloat16"),
    "gl": ("sbuf", [128, 6 * B], "bfloat16"),
    "pl": ("sbuf", [128, 3 * B], "bfloat16"),
    "sl": ("sbuf", [128, B], "bfloat16"),
    "t0": ("sbuf", [128, B], "float32"),
    "t1": ("sbuf", [128, B], "float32"),
    "dxs": ("sbuf", [128, B], "bfloat16"),
    "dws": ("sbuf", [128, B], "bfloat16"),
    "pf0": ("psum", [128, 512], "float32"),
    "pf1": ("psum", [128, 512], "float32"),
    "pn": ("psum", [128, 512], "float32"),
    "pt": ("psum", [128, 512], "float32"),
    "pw": ("psum", [128, 512], "float32"),
}
SEMAPHORES = (["xl", "wl", "dy0", "dy1", "dyn", "dtn", "dtf", "mf0", "mf1", "mn", "mw", "cf0", "cf1", "cn", "cw", "cx",
               "v0", "v1", "v2", "ga", "pa", "sa", "stx", "stw", "sent"]
              + ["xa%d" % s for s in range(8)] + ["xb%d" % s for s in range(8)])


def _bits(m):
    return [1 << i for i in range(m.bit_length()) if (m >> i) & 1]


def _join(bs):
    r = 0
    for b in bs:
        r |= b
    return r


def _layout(T, topo):
    cores = list(T.cores)
    chips = sorted(set(topo.chip(c) for c in cores))
    mem = dict((ch, [c for c in cores if topo.chip(c) == ch]) for ch in chips)
    far = {chips[0]: chips[1], chips[1]: chips[0]}
    gate, inner, slot = {}, {}, {}
    dies = sorted(set(topo.die(c) for c in cores))
    for i, ch in enumerate(chips):
        for c in mem[ch]:
            ok = all(topo.may_write(c, f) for f in mem[far[ch]])
            (gate if ok else inner)[(ch, topo.die(c))] = c
        for k, x in enumerate(dies):
            slot[inner[(ch, x)]] = 4 * i + 2 * k
            slot[gate[(ch, x)]] = 4 * i + 2 * k + 1
    return dict(mem=mem, far=far, gate=gate, inner=inner, slot=slot, dies=dies)


def _calls(c, L, topo):
    mem, gate, inner, slot, dies = L["mem"], L["gate"], L["inner"], L["slot"], L["dies"]
    ch, d = topo.chip(c), topo.die(c)
    fch = L["far"][ch]
    od = [x for x in dies if x != d][0]
    kd, ko = dies.index(d), dies.index(od)
    mates = [m for m in mem[ch] if m != c]
    I, G = inner[(ch, d)], gate[(ch, d)]
    FI, FG = inner[(fch, d)], gate[(fch, d)]
    on = _bits(topo.mask(c, mates[0]))

    def idx(dst, src):
        return [m for m in mem[topo.chip(dst)] if m != dst].index(src)

    def xt(s, n):
        return ("xs", B * s, B * (s + n))

    def cp(s, n, dsts, eng):
        return ([xt(s, n)], [(m,) + xt(s, n) for m in dsts], _join(eng), ("xa%d" if n == 1 else "xb%d") % s, 0)

    def grp(k, eng):
        gt = gate[(ch, dies[k])]
        j = idx(gt, c)
        return ([("ps", 2 * B * k, 2 * B * (k + 1))], [(gt, "gl", 2 * B * j, 2 * B * (j + 1))], _join(eng), "ga", 0)

    def near(eng):
        h = len(eng) // 2
        parts = [eng[:h], eng[h:h + h // 2], eng[h + h // 2:]]
        return [([("ps", B * (4 + mem[ch].index(m)), B * (5 + mem[ch].index(m)))],
                 [(m, "pl", B * idx(m, c), B * (idx(m, c) + 1))], _join(p), "pa", 0) for m, p in zip(mates, parts)]

    if G == c:
        out = _bits(topo.mask(c, FI))
        loc = [b for b in on if b not in out]
        h = len(out) // 2
        fg = [r for r in mem[fch] if topo.die(r) == d]
        folds = [([("gl", B * (2 * j + p), B * (2 * j + p + 1)) for j in range(3)]
                  + [("ps", B * (2 * kd + p), B * (2 * kd + p + 1))],
                  [(r, "sl", 0, B)], _join(e), "sa", 1) for p, (r, e) in enumerate(zip(fg, (out[:h], out[h:])))]
        return [
            ([("xl", 16)], [cp(slot[c], 1, [FI], out), cp(slot[c], 1, [I], loc)]),
            ([("cf%d" % ko, 1)], [grp(ko, loc)]),
            ([("xa%d" % slot[I], None)], [cp(slot[I], 1, [FI], out)]),
            ([("cn", 1)], near(loc)),
            ([("ga", None), ("cf%d" % kd, 1)], folds),
        ]
    ea, eb = on[0::2], on[1::2]
    return [
        ([("xl", 16)], [cp(slot[c], 1, [G], eb)]),
        ([("cf%d" % ko, 1), ("cf%d" % kd, 1)], [grp(ko, ea), grp(kd, eb)]),
        ([("xa%d" % slot[G], None)], [cp(slot[c], 2, [m for m in mates if topo.die(m) == od], on)]),
        ([("cn", 1)], near(on)),
        ([("xa%d" % slot[FG], None), ("xa%d" % slot[FI], None)], [cp(slot[FI], 2, mates, on)]),
    ]


def rank_program(g, core, T, topo):
    rank = T.rank_of(core)
    if rank is None:
        return
    L = _layout(T, topo)
    mem, gate, inner, slot, dies = L["mem"], L["gate"], L["inner"], L["slot"], L["dies"]
    ch, d = topo.chip(core), topo.die(core)
    fch = L["far"][ch]
    od = [x for x in dies if x != d][0]
    kd, ko = dies.index(d), dies.index(od)
    is_gate = gate[(ch, d)] == core
    S = T.sem
    te, ve, sy, sc = g.tensor, g.vector, g.sync, g.scalar

    arr, sent = {}, 0
    for c in T.cores:
        for _, trs in _calls(c, L, topo):
            for _, dsts, mask, sem, _ in trs:
                n = len(_bits(mask))
                if c == core:
                    sent += n
                for dst in dsts:
                    arr[(dst[0], sem)] = arr.get((dst[0], sem), 0) + n

    def cols(cs):
        ranks = [T.rank_of(c) for c in cs]
        lo = min(ranks)
        assert ranks == list(range(lo, lo + len(ranks)))
        return slice(B * lo, B * (lo + len(ranks)))

    cnear, cfar = cols(mem[ch]), cols(mem[fch])
    cf = [cols([r for r in mem[fch] if topo.die(r) == x]) for x in dies]
    by_slot = dict((s, c) for c, s in slot.items())

    def xs(s):
        return T.xs[:, B * s:B * (s + 1)]

    def dyt(s):
        r = T.rank_of(by_slot[s])
        return T.dyts[:, B * r:B * (r + 1)]

    sy.dma_start(xs(slot[core]), T.x[:]).then_inc(S.xl, 16)
    sc.dma_start(T.wts[:], T.wt[:]).then_inc(S.wl, 16)
    sy.dma_start(T.dys[:, cf[ko]], T.dy[:, cf[ko]]).then_inc(S["dy%d" % ko], 16)
    sc.dma_start(T.dys[:, cf[kd]], T.dy[:, cf[kd]]).then_inc(S["dy%d" % kd], 16)
    sy.dma_start(T.dys[:, cnear], T.dy[:, cnear]).then_inc(S.dyn, 16)
    sc.dma_start(T.dyts[:, cnear], T.dyt[:, cnear]).then_inc(S.dtn, 16)
    sy.dma_start(T.dyts[:, cfar], T.dyt[:, cfar]).then_inc(S.dtf, 16)

    te.wait_ge(S.wl, 16)
    for k in (ko, kd):
        te.wait_ge(S["dy%d" % k], 16)
        te.matmul(T["pf%d" % k][:, 0:2 * B], T.wts[:], T.dys[:, cf[k]], True, True).then_inc(S["mf%d" % k], 1)
    te.wait_ge(S.dyn, 16)
    te.matmul(T.pn[:, 0:4 * B], T.wts[:], T.dys[:, cnear], True, True).then_inc(S.mn, 1)

    sI, sG = slot[inner[(ch, d)]], slot[gate[(ch, d)]]
    sO = slot[inner[(ch, od)]]
    fD, fO = slot[inner[(fch, d)]], slot[inner[(fch, od)]]
    if is_gate:
        due = [("xa%d" % sI, [sI]), ("xb%d" % sO, [sO, sO + 1]), ("xb%d" % fD, [fD, fD + 1]),
               ("xb%d" % fO, [fO, fO + 1])]
    else:
        due = [("xa%d" % sG, [sG]), ("xb%d" % sO, [sO, sO + 1]), ("xa%d" % (fD + 1), [fD + 1]), ("xa%d" % fD, [fD]),
               ("xb%d" % fO, [fO, fO + 1])]
    te.wait_ge(S.xl, 16)
    te.wait_ge(S.dtn, 16)
    te.matmul(T.pw[:, 0:B], xs(slot[core]), dyt(slot[core]), True, False)
    far_seen = False
    for n, (sem, ss) in enumerate(due):
        if not far_seen and topo.chip(by_slot[ss[0]]) != ch:
            te.wait_ge(S.dtf, 16)
            far_seen = True
        te.wait_ge(S[sem], arr[(core, sem)])
        for s in ss:
            mm = te.matmul(T.pw[:, 0:B], xs(s), dyt(s), False, n == len(due) - 1 and s == ss[-1])
    mm.then_inc(S.mw, 1)

    for k in (ko, kd):
        ve.wait_ge(S["mf%d" % k], 1)
        ve.tensor_copy(T.ps[:, 2 * B * k:2 * B * (k + 1)], T["pf%d" % k][:, 0:2 * B]).then_inc(S["cf%d" % k], 1)
    ve.wait_ge(S.mn, 1)
    ve.tensor_copy(T.ps[:, 4 * B:8 * B], T.pn[:, 0:4 * B]).then_inc(S.cn, 1)
    own = mem[ch].index(core)
    ve.wait_ge(S.pa, arr[(core, "pa")])
    ve.tensor_tensor(T.t0[:], T.pn[:, B * own:B * (own + 1)], T.pl[:, 0:B], AluOpType.add).then_inc(S.v0, 1)
    ve.tensor_tensor(T.t1[:], T.pl[:, B:2 * B], T.pl[:, 2 * B:3 * B], AluOpType.add).then_inc(S.v1, 1)
    ve.wait_ge(S.v0, 1)
    ve.wait_ge(S.v1, 1)
    ve.tensor_tensor(T.pt[:, 0:B], T.t0[:], T.t1[:], AluOpType.add).then_inc(S.v2, 1)
    ve.wait_ge(S.v2, 1)
    ve.wait_ge(S.sa, arr[(core, "sa")])
    ve.tensor_tensor(T.dxs[:], T.pt[:, 0:B], T.sl[:], AluOpType.add).then_inc(S.cx, 1)

    sc.wait_ge(S.mw, 1)
    sc.activation(T.dws[:], T.pw[:, 0:B], ActivationFunctionType.Copy).then_inc(S.cw, 1)
    sc.wait_ge(S.cw, 1)
    sc.dma_start(T.dw[:], T.dws[:]).then_inc(S.stw, 16)
    sc.wait_ge(S.stw, 16)
    sy.wait_ge(S.cx, 1)
    sy.dma_start(T.dx[:], T.dxs[:]).then_inc(S.stx, 16)
    sy.wait_ge(S.stx, 16)

    def ap(spec):
        return T[spec[0]][:, spec[1]:spec[2]]

    for waits, trs in _calls(core, L, topo):
        for sem, val in waits:
            g.wait_ge(S[sem], arr[(core, sem)] if val is None else val)
        g.remote_dma_fused(
            [RemoteDMATransfer(dst_ids=[DstId(rid=topo.addr(t[0])[0], pnc=topo.addr(t[0])[1]) for t in dsts],
                               dma_engine_mask=mask, remote_sem=S[sem], srcs=[ap(s) for s in srcs],
                               dsts=[ap(t[1:]) for t in dsts], alu_op=alu)
             for srcs, dsts, mask, sem, alu in trs], local_sem=S.sent)
    g.wait_ge(S.sent, sent)
